import numpy as np
import ml_dtypes


def mxq(x, axis, fmt="e4m3"):
    dtype, down = {"e4m3": (ml_dtypes.float8_e4m3fn, 7), "e5m2": (ml_dtypes.float8_e5m2, 14)}[fmt]
    v = np.moveaxis(np.asarray(x, np.float32).astype(ml_dtypes.bfloat16).astype(np.float64), axis, -1)
    blocks = v.reshape(v.shape[:-1] + (-1, 32))
    amax = np.abs(blocks).max(-1, keepdims=True)
    byte = np.maximum(np.where(amax > 0, np.frexp(amax)[1] - 1 + 127, 0) - down, 1)
    scale = np.exp2(byte - 127.0)
    codes = (blocks / scale).astype(np.float32).astype(dtype).astype(np.float64)
    return np.moveaxis((codes * scale).reshape(v.shape), -1, axis)


WIDE = False


def mx_kscale(k):
    if not WIDE:
        return np.ones(k)
    levels = np.array([10, -10, 5, -5, 0])
    if k % 512:
        return np.exp2(np.random.permutation(np.resize(levels, k // 32))).repeat(32)
    a = np.empty((k // 512, 16))
    for p in range(k // 512):
        a[p, :8] = np.random.permutation(np.resize(levels, 8))
        for g in range(8):
            far = levels[np.abs(levels - a[p, g]) >= 10]
            a[p, g + 8] = far[np.random.randint(len(far))]
    return np.exp2(a.ravel()).repeat(32)


def f64(x):
    return np.asarray(x).astype(np.float64)


def striped(idx):
    return np.tile(idx.reshape(-1, 16).T, (8, 1)).astype(np.uint16)


def unstriped(offs):
    return offs[:16].T.reshape(-1).astype(np.int64)


def striped8(idx):
    return np.concatenate([x.reshape(-1, 16).T for x in idx]).astype(np.uint16)


def runs(offs, k):
    lists = np.stack([offs[16 * r : 16 * r + 16].T.reshape(-1) for r in range(8)]).astype(np.int64)
    return lists[np.arange(k) % 512 // 64]


def pack_weight(w):
    k, n = w.shape
    w = f64(np.asarray(w, np.float32).astype(ml_dtypes.bfloat16)).reshape(k // 32, 32, n)
    amax = np.abs(w).max(1)
    byte = np.clip(np.where(amax > 0, np.frexp(amax)[1] - 1 + 127 - 7, 1), 1, 254)
    scaled = (w * np.exp2(127.0 - byte)[:, None, :]).reshape(k, n).astype(np.float32)
    words = np.ascontiguousarray(scaled.reshape(k // 512, 128, 4, n).transpose(0, 1, 3, 2)).astype(ml_dtypes.float8_e4m3fn).view(np.uint8)
    return words, np.ascontiguousarray(byte.astype(np.uint8).reshape(k // 512, 16, n))


def unpack_weight(words, scales):
    g, p, n, _ = words.shape
    vals = np.ascontiguousarray(words).view(ml_dtypes.float8_e4m3fn).astype(np.float64) * np.repeat(np.exp2(scales.astype(np.float64) - 127.0), 8, axis=1)[..., None]
    return vals.transpose(0, 1, 3, 2).reshape(g * 512, n)


def sigmoid(v):
    return 1.0 / (1.0 + np.exp(-np.maximum(v, -700.0)))


K, T, S, N, H = 512, 2048, 512, 512, 512


def setup_inputs():
    n = np.random.standard_normal
    s = mx_kscale(K)[:, None]
    u = mx_kscale(H)
    packed_xT = pack_weight(n((K, T)) * s)
    return {
        "x_words": packed_xT[0],
        "x_scales": packed_xT[1],
        "w1": (n((K, H)) / np.sqrt(K) / s).astype(np.float32),
        "gn": (np.random.uniform(0.5, 1.5, (H, 1)) * u[:, None]).astype(np.float32),
        "w2": (n((H, N)) / np.sqrt(H) / u[:, None]).astype(np.float32),
        "offs": striped(np.random.permutation(T)[:S]),
        "n1": striped8(np.stack([np.random.permutation(S) for _ in range(8)])),
        "n2": striped8(np.stack([np.random.permutation(S) for _ in range(8)])),
        "n3": striped8(np.stack([np.random.permutation(S) for _ in range(8)])),
        "n4": striped8(np.stack([np.random.permutation(S) for _ in range(8)])),
    }


def reference(x_words, x_scales, w1, gn, w2, offs, n1, n2, n3, n4):
    xq = unpack_weight(x_words, x_scales)[:, unstriped(offs)]
    y = mxq(f64(w1), 0, "e4m3").T @ xq
    z = f64(gn) * ((y - (y[np.arange(H)[:, None], runs(n1, H)])) / (np.abs(y[np.arange(H)[:, None], runs(n2, H)] - y) + 0.5))
    h = mxq(f64(w2), 0, "e4m3").T @ mxq(z, 0, "e4m3")
    return h + (sigmoid(y[np.arange(H)[:, None], runs(n4, H)] - y)) * (h[np.arange(N)[:, None], runs(n3, N)] - h)

@@ -1,0 +1,214 @@
+from contextlib import ExitStack
+
+import concourse.mybir as mybir
+from concourse.masks import make_identity
+
+K, T, S, N, H = 512, 2048, 512, 512, 512
+FLOPS = 2 * K * H * S + 2 * H * N * S
+
+F32 = mybir.dt.float32
+BF16 = mybir.dt.bfloat16
+I32 = mybir.dt.int32
+U32 = mybir.dt.uint32
+U16 = mybir.dt.uint16
+U8 = mybir.dt.uint8
+FP8X4 = mybir.dt.float8_e4m3fn_x4
+ALU = mybir.AluOpType
+ACT = mybir.ActivationFunctionType
+
+P = 128
+PACK = 4
+HALF = S // 2
+LIST_COLS = S // 16
+
+
+def tile_picked_skippullbfrac_none_p_kernel(tc, x_words, x_scales, w1, gn, w2, offs, n1, n2, n3, n4, out):
+    nc = tc.nc
+    with ExitStack() as ctx:
+        keep = ctx.enter_context(tc.tile_pool(name="keep", bufs=1))
+        psum = ctx.enter_context(tc.psum_pool(name="psum", bufs=1))
+
+        def load_list(src, name):
+            tile = keep.tile([P, LIST_COLS], U16, name=name)
+            nc.sync.dma_start(tile[:], src)
+            return tile
+
+        def cols(half):
+            return slice(half * HALF, (half + 1) * HALF)
+
+        def entries(tile, half):
+            return tile[:, half * HALF // 16 : (half + 1) * HALF // 16]
+
+        xs_all = keep.tile([P, T], U8, name="xs_all")
+        nc.vector.memset(xs_all[:].bitcast(I32), 0)
+        offs_t = load_list(offs, "offs_t")
+        w1_raw = [keep.tile([P, PACK, H // 2], F32, name="w1_raw%d" % c) for c in range(2)]
+        w1_rows = w1.rearrange("(p j) c -> p j c", j=PACK)
+        for c in range(2):
+            nc.sync.dma_start(w1_raw[c][:], w1_rows[:, :, c * (H // 2) : (c + 1) * (H // 2)])
+        for q in range(4):
+            nc.scalar.dma_start(xs_all[32 * q : 32 * q + 4, :].bitcast(I32), x_scales[0, 4 * q : 4 * q + 4, :].bitcast(I32))
+        xw_all = keep.tile([P, T], I32, name="xw_all")
+        nc.sync.dma_start(xw_all[:], x_words[0].rearrange("p c r -> p (c r)").bitcast(I32))
+        n2_t = load_list(n2, "n2_t")
+        n1_t = load_list(n1, "n1_t")
+        n4_t = load_list(n4, "n4_t")
+        gn_t = keep.tile([P, PACK], F32, name="gn_t")
+        nc.sync.dma_start(gn_t[:], gn.rearrange("(p t) o -> p (t o)", t=PACK))
+        w2_raw = [keep.tile([P, PACK, N // 2], F32, name="w2_raw%d" % c) for c in range(2)]
+        w2_rows = w2.rearrange("(p j) c -> p j c", j=PACK)
+        for c in range(2):
+            nc.sync.dma_start(w2_raw[c][:], w2_rows[:, :, c * (N // 2) : (c + 1) * (N // 2)])
+        n3_t = load_list(n3, "n3_t")
+
+        w1_bf = keep.tile([P, H * PACK], BF16, name="w1_bf", align_bytes=64)
+        w1_dealt = w1_bf[:].rearrange("p (t m j) -> p m t j", t=PACK, j=PACK)
+        for c in range(2):
+            nc.vector.tensor_copy(out=w1_dealt[:, c * 64 : (c + 1) * 64, :, :], in_=w1_raw[c][:].rearrange("p j (m t) -> p m t j", t=PACK))
+        xs_g = keep.tile([P, S], U8, name="xs_g", align_bytes=64)
+        nc.vector.tensor_copy(out=xs_g[:], in_=xs_all[:].indirect(offs_t[:]))
+        w1_q = keep.tile([P, H], U32, name="w1_q", align_bytes=64)
+        w1_s = keep.tile([P, H], U8, name="w1_s", align_bytes=64)
+        nc.vector.quantize_mx(out=w1_q[:].bitcast(FP8X4), scales=w1_s[:], in_=w1_bf[:])
+        xw_g = [keep.tile([P, HALF], U32, name="xw_g%d" % c, align_bytes=64) for c in range(2)]
+        y_win = [keep.tile([P, S], F32, name="y_win%d" % t) for t in range(PACK)]
+        y_cp = keep.tile([P, PACK, S], F32, name="y_cp")
+        for half in range(2):
+            nc.vector.tensor_copy(out=xw_g[half][:], in_=xw_all[:].bitcast(U32).indirect(entries(offs_t, half)))
+            for pair in range(2):
+                bank = psum.tile([P, 2, HALF], F32, name="y_bank", tag="turn%d" % (2 * half + pair))
+                for i in range(2):
+                    m = slice((2 * pair + i) * P, (2 * pair + i + 1) * P)
+                    nc.tensor.matmul_mx(out=bank[:, i, :], lhsT=w1_q[:, m].bitcast(FP8X4), lhsT_scale=w1_s[:, m], rhs=xw_g[half][:].bitcast(FP8X4), rhs_scale=xs_g[:, cols(half)], start=True, stop=True)
+                for i in range(2):
+                    nc.scalar.copy(out=y_win[2 * pair + i][:, cols(half)], in_=bank[:, i, :])
+
+        ident = keep.tile([P, P], F32, name="ident")
+        make_identity(nc, ident[:])
+        neg_gn = keep.tile([P, PACK], F32, name="neg_gn")
+        nc.vector.tensor_scalar(out=neg_gn[:], in0=gn_t[:], scalar1=-1.0, scalar2=None, op0=ALU.mult)
+
+        d1 = keep.tile([P, PACK, S], F32, name="d1")
+        d2 = keep.tile([P, PACK, S], F32, name="d2")
+        d4 = [keep.tile([P, S], F32, name="d4", tag="row%d" % t) for t in range(PACK)]
+        mag = keep.tile([P, PACK, S], F32, name="mag")
+        root = keep.tile([P, PACK, S], F32, name="root")
+        half_bias = keep.tile([P, 1], F32, name="half_bias")
+        nc.vector.memset(half_bias[:], 0.5)
+
+        def diff(dst, lst, t, half):
+            nc.vector.tensor_tensor(out=dst[:, t, cols(half)], in0=y_win[t][:].indirect(entries(lst, half)), in1=y_cp[:, t, cols(half)], op=ALU.subtract)
+
+        def fetch4(pair):
+            for t, half in ((2 * pair, 0), (2 * pair, 1), (2 * pair + 1, 0), (2 * pair + 1, 1)):
+                nc.scalar.activation(out=d4[t][:, cols(half)], in_=y_win[t][:].indirect(entries(n4_t, half)), func=ACT.Copy, scale=-1.0)
+
+        def denominators(half):
+            nc.scalar.activation(out=mag[:, :, cols(half)], in_=d2[:, :, cols(half)], func=ACT.Abs)
+            nc.scalar.activation(out=root[:, :, cols(half)], in_=mag[:, :, cols(half)], func=ACT.Abs_reciprocal_sqrt, bias=half_bias[:])
+
+        z_bf = [keep.tile([P, HALF * PACK], BF16, name="z_bf%d" % c, align_bytes=64) for c in range(2)]
+        z_q = [keep.tile([P, HALF], U32, name="z_q%d" % c, align_bytes=64) for c in range(2)]
+        z_s = [keep.tile([P, HALF], U8, name="z_s%d" % c, align_bytes=64) for c in range(2)]
+
+        def make_z(half):
+            for t in range(PACK):
+                nc.vector.scalar_tensor_tensor(out=d1[:, t, cols(half)], in0=d1[:, t, cols(half)], scalar=neg_gn[:, t : t + 1], in1=root[:, t, cols(half)], op0=ALU.mult, op1=ALU.mult)
+            nc.vector.tensor_tensor(
+                out=z_bf[half][:].rearrange("p (c i t) -> p c t i", i=4, t=PACK),
+                in0=d1[:, :, cols(half)].rearrange("p t (c i) -> p c t i", i=4),
+                in1=root[:, :, cols(half)].rearrange("p t (c i) -> p c t i", i=4),
+                op=ALU.mult,
+            )
+
+        def quantise_z(half):
+            nc.vector.quantize_mx(out=z_q[half][:].bitcast(FP8X4), scales=z_s[half][:], in_=z_bf[half][:])
+
+        w2_bf = keep.tile([P, N * PACK], BF16, name="w2_bf", align_bytes=64)
+        w2_q = keep.tile([P, N], U32, name="w2_q", align_bytes=64)
+        w2_s = keep.tile([P, N], U8, name="w2_s", align_bytes=64)
+        h_win = []
+        h_bank = {}
+
+        def second_product(half):
+            for pair in range(2):
+                bank = psum.tile([P, 2, HALF], F32, name="h_bank%d%d" % (half, pair))
+                h_bank[half, pair] = bank
+                for i in range(2):
+                    m = slice((2 * pair + i) * P, (2 * pair + i + 1) * P)
+                    nc.tensor.matmul_mx(out=bank[:, i, :], lhsT=w2_q[:, m].bitcast(FP8X4), lhsT_scale=w2_s[:, m], rhs=z_q[half][:].bitcast(FP8X4), rhs_scale=z_s[half][:], start=True, stop=True)
+            for t in range(PACK):
+                nc.scalar.copy(out=h_win[t][:, cols(half)], in_=h_bank[half, t // 2][:, t % 2, :])
+
+        def negate(t, half):
+            if half == 0:
+                nc.vector.tensor_copy(out=y_cp[:, t, cols(half)], in_=y_win[t][:, cols(half)])
+            else:
+                nc.sync.dma_start(y_cp[:, t, cols(half)], y_win[t][:, cols(half)])
+
+        gate = []
+
+        def make_gate(t):
+            turned = psum.tile([P, S], F32, name="turned", tag="turn%d" % t)
+            for k, src in enumerate((y_win[t], d4[t])):
+                for b in range(S // P):
+                    blk = slice(b * P, (b + 1) * P)
+                    nc.tensor.matmul(out=turned[:, blk], lhsT=src[:, blk], rhs=ident[:], start=(k == 0 and b == 0), stop=(k == 1 and b == S // P - 1), is_transpose=True)
+            nc.scalar.activation(out=mag[:, t, :], in_=turned[:], func=ACT.Sigmoid, scale=-1.0)
+            back = psum.tile([P, S], F32, name="gate", tag="turn%d" % t)
+            for b in range(S // P):
+                blk = slice(b * P, (b + 1) * P)
+                nc.tensor.transpose(back[:, blk], mag[:, t, blk], ident[:])
+            gate.append(back)
+
+        for t in range(PACK):
+            negate(t, 0)
+        for t in range(PACK):
+            negate(t, 1)
+        for t in range(PACK):
+            diff(d2, n2_t, t, 0)
+        denominators(0)
+        for t in range(PACK):
+            diff(d1, n1_t, t, 0)
+        for t in range(PACK):
+            diff(d2, n2_t, t, 1)
+        denominators(1)
+        fetch4(0)
+        fetch4(1)
+        w2_dealt = w2_bf[:].rearrange("p (t m j) -> p m t j", t=PACK, j=PACK)
+        for c in range(2):
+            nc.vector.tensor_copy(out=w2_dealt[:, c * 64 : (c + 1) * 64, :, :], in_=w2_raw[c][:].rearrange("p j (m t) -> p m t j", t=PACK))
+        make_z(0)
+        nc.vector.quantize_mx(out=w2_q[:].bitcast(FP8X4), scales=w2_s[:], in_=w2_bf[:])
+        quantise_z(0)
+        for t in range(PACK):
+            diff(d1, n1_t, t, 1)
+        make_z(1)
+        for t in range(PACK):
+            make_gate(t)
+        for t in range(PACK):
+            h_win.append(keep.tile([P, S], F32, name="h_win", tag="row%d" % ((t + 3) % PACK)))
+        second_product(0)
+        quantise_z(1)
+        second_product(1)
+
+        stay = keep.tile([P, PACK, S], F32, name="stay")
+        for half in range(2):
+            for t in range(PACK):
+                nc.vector.scalar_tensor_tensor(out=stay[:, t, cols(half)], in0=gate[t][:, cols(half)], scalar=1.0, in1=h_win[t][:, cols(half)], op0=ALU.subtract, op1=ALU.mult)
+        pull = keep.tile([P, PACK, S], F32, name="pull")
+        res = [keep.tile([P, S], F32, name="res%d" % t) for t in range(PACK)]
+        out_rows = out.rearrange("(p t) c -> p t c", t=PACK)
+        for t in range(PACK):
+            for half in range(2):
+                c = cols(half)
+                if t == -1:
+                    nc.vector.tensor_copy(out=pull[:, t, c], in_=h_win[t][:].indirect(entries(n3_t, half)))
+                else:
+                    nc.scalar.activation(out=pull[:, t, c], in_=h_win[t][:].indirect(entries(n3_t, half)), func=ACT.Copy)
+        for t in range(PACK):
+            for c in (cols(0), cols(1)):
+                nc.vector.tensor_tensor(out=pull[:, t, c], in0=pull[:, t, c], in1=gate[t][:, c], op=ALU.mult)
+            for c in (cols(0), cols(1)):
+                (nc.gpsimd if t in () else nc.vector).tensor_tensor(out=res[t][:, c], in0=pull[:, t, c], in1=stay[:, t, c], op=ALU.subtract)
+            nc.sync.dma_start(out_rows[:, t, :], res[t][:])

@@ -47,7 +47,7 @@ def tile_picked_skippullbfrac_none_p_kernel(tc, x_words, x_scales, w1, gn, w2, o
         for c in range(2):
             nc.sync.dma_start(w1_raw[c][:], w1_rows[:, :, c * (H // 2) : (c + 1) * (H // 2)])
         for q in range(4):
-            nc.scalar.dma_start(xs_all[32 * q : 32 * q + 4, :].bitcast(I32), x_scales[0, 4 * q : 4 * q + 4, :].bitcast(I32))
+            nc.sync.dma_start(xs_all[32 * q : 32 * q + 4, :].bitcast(I32), x_scales[0, 4 * q : 4 * q + 4, :].bitcast(I32))
         xw_all = keep.tile([P, T], I32, name="xw_all")
         nc.sync.dma_start(xw_all[:], x_words[0].rearrange("p c r -> p (c r)").bitcast(I32))
         n2_t = load_list(n2, "n2_t")
@@ -55,10 +55,9 @@ def tile_picked_skippullbfrac_none_p_kernel(tc, x_words, x_scales, w1, gn, w2, o
         n4_t = load_list(n4, "n4_t")
         gn_t = keep.tile([P, PACK], F32, name="gn_t")
         nc.sync.dma_start(gn_t[:], gn.rearrange("(p t) o -> p (t o)", t=PACK))
-        w2_raw = [keep.tile([P, PACK, N // 2], F32, name="w2_raw%d" % c) for c in range(2)]
+        w2_raw = [keep.tile([P, PACK, N // 2], F32, name="w2_raw%d" % c, tag="w2_raw") for c in range(1)]
         w2_rows = w2.rearrange("(p j) c -> p j c", j=PACK)
-        for c in range(2):
-            nc.sync.dma_start(w2_raw[c][:], w2_rows[:, :, c * (N // 2) : (c + 1) * (N // 2)])
+        nc.sync.dma_start(w2_raw[0][:], w2_rows[:, :, : N // 2])
         n3_t = load_list(n3, "n3_t")
 
         w1_bf = keep.tile([P, H * PACK], BF16, name="w1_bf", align_bytes=64)
@@ -67,21 +66,19 @@ def tile_picked_skippullbfrac_none_p_kernel(tc, x_words, x_scales, w1, gn, w2, o
             nc.vector.tensor_copy(out=w1_dealt[:, c * 64 : (c + 1) * 64, :, :], in_=w1_raw[c][:].rearrange("p j (m t) -> p m t j", t=PACK))
         xs_g = keep.tile([P, S], U8, name="xs_g", align_bytes=64)
         nc.vector.tensor_copy(out=xs_g[:], in_=xs_all[:].indirect(offs_t[:]))
-        w1_q = keep.tile([P, H], U32, name="w1_q", align_bytes=64)
-        w1_s = keep.tile([P, H], U8, name="w1_s", align_bytes=64)
+        w1_q = keep.tile([P, H], U32, name="w1_q", tag="row0", align_bytes=64)
+        w1_s = keep.tile([P, H], U8, name="w1_s", tag="row1", align_bytes=64)
         nc.vector.quantize_mx(out=w1_q[:].bitcast(FP8X4), scales=w1_s[:], in_=w1_bf[:])
         xw_g = [keep.tile([P, HALF], U32, name="xw_g%d" % c, align_bytes=64) for c in range(2)]
         y_win = [keep.tile([P, S], F32, name="y_win%d" % t) for t in range(PACK)]
         y_cp = keep.tile([P, PACK, S], F32, name="y_cp")
         for half in range(2):
             nc.vector.tensor_copy(out=xw_g[half][:], in_=xw_all[:].bitcast(U32).indirect(entries(offs_t, half)))
-            for pair in range(2):
-                bank = psum.tile([P, 2, HALF], F32, name="y_bank", tag="turn%d" % (2 * half + pair))
-                for i in range(2):
-                    m = slice((2 * pair + i) * P, (2 * pair + i + 1) * P)
-                    nc.tensor.matmul_mx(out=bank[:, i, :], lhsT=w1_q[:, m].bitcast(FP8X4), lhsT_scale=w1_s[:, m], rhs=xw_g[half][:].bitcast(FP8X4), rhs_scale=xs_g[:, cols(half)], start=True, stop=True)
-                for i in range(2):
-                    nc.scalar.copy(out=y_win[2 * pair + i][:, cols(half)], in_=bank[:, i, :])
+        for t, half in ((0, 0), (1, 0), (0, 1), (1, 1), (2, 0), (2, 1), (3, 0), (3, 1)):
+            bank = psum.tile([P, HALF], F32, name="y_bank", tag=("turn%d" % t if half == 0 else "side%d" % t))
+            m = slice(t * P, (t + 1) * P)
+            nc.tensor.matmul_mx(out=bank[:], lhsT=w1_q[:, m].bitcast(FP8X4), lhsT_scale=w1_s[:, m], rhs=xw_g[half][:].bitcast(FP8X4), rhs_scale=xs_g[:, cols(half)], start=True, stop=True)
+            nc.scalar.copy(out=y_win[t][:, cols(half)], in_=bank[:])
 
         ident = keep.tile([P, P], F32, name="ident")
         make_identity(nc, ident[:])
@@ -90,11 +87,14 @@ def tile_picked_skippullbfrac_none_p_kernel(tc, x_words, x_scales, w1, gn, w2, o
 
         d1 = keep.tile([P, PACK, S], F32, name="d1")
         d2 = keep.tile([P, PACK, S], F32, name="d2")
-        d4 = [keep.tile([P, S], F32, name="d4", tag="row%d" % t) for t in range(PACK)]
-        mag = keep.tile([P, PACK, S], F32, name="mag")
-        root = keep.tile([P, PACK, S], F32, name="root")
+        d4 = [keep.tile([P, S], F32, name="d4", tag="row%d" % t, align_bytes=64) for t in range(PACK)]
+        mag = [keep.tile([P, PACK, HALF], F32, name="mag", tag="mag%d" % c, align_bytes=64) for c in range(2)]
+        root = [keep.tile([P, PACK, HALF], F32, name="root", tag="root%d" % c) for c in range(2)]
         half_bias = keep.tile([P, 1], F32, name="half_bias")
         nc.vector.memset(half_bias[:], 0.5)
+
+        warm = keep.tile([P, 1], F32, name="warm")
+        nc.scalar.activation(out=warm[:], in_=half_bias[:], func=ACT.Abs_reciprocal_sqrt)
 
         def diff(dst, lst, t, half):
             nc.vector.tensor_tensor(out=dst[:, t, cols(half)], in0=y_win[t][:].indirect(entries(lst, half)), in1=y_cp[:, t, cols(half)], op=ALU.subtract)
@@ -104,8 +104,8 @@ def tile_picked_skippullbfrac_none_p_kernel(tc, x_words, x_scales, w1, gn, w2, o
                 nc.scalar.activation(out=d4[t][:, cols(half)], in_=y_win[t][:].indirect(entries(n4_t, half)), func=ACT.Copy, scale=-1.0)
 
         def denominators(half):
-            nc.scalar.activation(out=mag[:, :, cols(half)], in_=d2[:, :, cols(half)], func=ACT.Abs)
-            nc.scalar.activation(out=root[:, :, cols(half)], in_=mag[:, :, cols(half)], func=ACT.Abs_reciprocal_sqrt, bias=half_bias[:])
+            nc.scalar.activation(out=mag[half][:], in_=d2[:, :, cols(half)], func=ACT.Abs)
+            nc.scalar.activation(out=root[half][:], in_=mag[half][:], func=ACT.Abs_reciprocal_sqrt, bias=half_bias[:])
 
         z_bf = [keep.tile([P, HALF * PACK], BF16, name="z_bf%d" % c, align_bytes=64) for c in range(2)]
         z_q = [keep.tile([P, HALF], U32, name="z_q%d" % c, align_bytes=64) for c in range(2)]
@@ -113,15 +113,17 @@ def tile_picked_skippullbfrac_none_p_kernel(tc, x_words, x_scales, w1, gn, w2, o
 
         def make_z(half):
             for t in range(PACK):
-                nc.vector.scalar_tensor_tensor(out=d1[:, t, cols(half)], in0=d1[:, t, cols(half)], scalar=neg_gn[:, t : t + 1], in1=root[:, t, cols(half)], op0=ALU.mult, op1=ALU.mult)
+                nc.vector.scalar_tensor_tensor(out=d1[:, t, cols(half)], in0=d1[:, t, cols(half)], scalar=neg_gn[:, t : t + 1], in1=root[half][:, t, :], op0=ALU.mult, op1=ALU.mult)
             nc.vector.tensor_tensor(
                 out=z_bf[half][:].rearrange("p (c i t) -> p c t i", i=4, t=PACK),
                 in0=d1[:, :, cols(half)].rearrange("p t (c i) -> p c t i", i=4),
-                in1=root[:, :, cols(half)].rearrange("p t (c i) -> p c t i", i=4),
+                in1=root[half][:].rearrange("p t (c i) -> p c t i", i=4),
                 op=ALU.mult,
             )
 
         def quantise_z(half):
+            if half == 1:
+                z_q[half] = keep.tile([P, HALF], U32, name="z_q_late", tag="mag1", align_bytes=64)
             nc.vector.quantize_mx(out=z_q[half][:].bitcast(FP8X4), scales=z_s[half][:], in_=z_bf[half][:])
 
         w2_bf = keep.tile([P, N * PACK], BF16, name="w2_bf", align_bytes=64)
@@ -131,14 +133,15 @@ def tile_picked_skippullbfrac_none_p_kernel(tc, x_words, x_scales, w1, gn, w2, o
         h_bank = {}
 
         def second_product(half):
-            for pair in range(2):
-                bank = psum.tile([P, 2, HALF], F32, name="h_bank%d%d" % (half, pair))
-                h_bank[half, pair] = bank
-                for i in range(2):
-                    m = slice((2 * pair + i) * P, (2 * pair + i + 1) * P)
+            per_bank = 2 - half
+            for first in range(0, PACK, per_bank):
+                bank = psum.tile([P, per_bank, HALF], F32, name="h_bank", tag="side%d" % (first // 2 if half == 0 else (first + 2) % PACK))
+                for i in range(per_bank):
+                    m = slice((first + i) * P, (first + i + 1) * P)
                     nc.tensor.matmul_mx(out=bank[:, i, :], lhsT=w2_q[:, m].bitcast(FP8X4), lhsT_scale=w2_s[:, m], rhs=z_q[half][:].bitcast(FP8X4), rhs_scale=z_s[half][:], start=True, stop=True)
-            for t in range(PACK):
-                nc.scalar.copy(out=h_win[t][:, cols(half)], in_=h_bank[half, t // 2][:, t % 2, :])
+                for i in range(per_bank):
+                    move = nc.vector.tensor_copy if half == 1 and first < 2 else nc.scalar.copy
+                    move(out=h_win[first + i][:, cols(half)], in_=bank[:, i, :])
 
         def negate(t, half):
             if half == 0:
@@ -148,17 +151,17 @@ def tile_picked_skippullbfrac_none_p_kernel(tc, x_words, x_scales, w1, gn, w2, o
 
         gate = []
 
-        def make_gate(t):
+        def make_gate(t, gate_t):
             turned = psum.tile([P, S], F32, name="turned", tag="turn%d" % t)
             for k, src in enumerate((y_win[t], d4[t])):
                 for b in range(S // P):
                     blk = slice(b * P, (b + 1) * P)
                     nc.tensor.matmul(out=turned[:, blk], lhsT=src[:, blk], rhs=ident[:], start=(k == 0 and b == 0), stop=(k == 1 and b == S // P - 1), is_transpose=True)
-            nc.scalar.activation(out=mag[:, t, :], in_=turned[:], func=ACT.Sigmoid, scale=-1.0)
+            nc.scalar.activation(out=gate_t[:, t % 2, :], in_=turned[:], func=ACT.Sigmoid, scale=-1.0)
             back = psum.tile([P, S], F32, name="gate", tag="turn%d" % t)
             for b in range(S // P):
                 blk = slice(b * P, (b + 1) * P)
-                nc.tensor.transpose(back[:, blk], mag[:, t, blk], ident[:])
+                nc.tensor.transpose(back[:, blk], gate_t[:, t % 2, blk], ident[:])
             gate.append(back)
 
         for t in range(PACK):
@@ -176,21 +179,28 @@ def tile_picked_skippullbfrac_none_p_kernel(tc, x_words, x_scales, w1, gn, w2, o
         fetch4(0)
         fetch4(1)
         w2_dealt = w2_bf[:].rearrange("p (t m j) -> p m t j", t=PACK, j=PACK)
-        for c in range(2):
-            nc.vector.tensor_copy(out=w2_dealt[:, c * 64 : (c + 1) * 64, :, :], in_=w2_raw[c][:].rearrange("p j (m t) -> p m t j", t=PACK))
+        for c, move in enumerate((nc.vector.tensor_copy, nc.scalar.copy)):
+            if c == 1:
+                w2_raw.append(keep.tile([P, PACK, N // 2], F32, name="w2_raw1", tag="w2_raw"))
+                nc.sync.dma_start(w2_raw[1][:], w2_rows[:, :, N // 2 :])
+            move(out=w2_dealt[:, c * 64 : (c + 1) * 64, :, :], in_=w2_raw[c][:].rearrange("p j (m t) -> p m t j", t=PACK))
         make_z(0)
         nc.vector.quantize_mx(out=w2_q[:].bitcast(FP8X4), scales=w2_s[:], in_=w2_bf[:])
         quantise_z(0)
         for t in range(PACK):
             diff(d1, n1_t, t, 1)
         make_z(1)
+        early = keep.tile([P, 2, S], F32, name="gate_t", tag="mag1", align_bytes=64)
+        for t in range(2):
+            make_gate(t, early)
         for t in range(PACK):
-            make_gate(t)
-        for t in range(PACK):
-            h_win.append(keep.tile([P, S], F32, name="h_win", tag="row%d" % ((t + 3) % PACK)))
+            h_win.append(keep.tile([P, S], F32, name="h_win", tag="win%d" % t))
         second_product(0)
         quantise_z(1)
         second_product(1)
+        late = keep.tile([P, 2, S], F32, name="gate_t", tag="root1")
+        for t in range(2, PACK):
+            make_gate(t, late)
 
         stay = keep.tile([P, PACK, S], F32, name="stay")
         for half in range(2):
@@ -211,4 +221,5 @@ def tile_picked_skippullbfrac_none_p_kernel(tc, x_words, x_scales, w1, gn, w2, o
                 nc.vector.tensor_tensor(out=pull[:, t, c], in0=pull[:, t, c], in1=gate[t][:, c], op=ALU.mult)
             for c in (cols(0), cols(1)):
                 (nc.gpsimd if t in () else nc.vector).tensor_tensor(out=res[t][:, c], in0=pull[:, t, c], in1=stay[:, t, c], op=ALU.subtract)
-            nc.sync.dma_start(out_rows[:, t, :], res[t][:])
+            for c in ((cols(0), cols(1)) if t >= 3 else (slice(0, S),)):
+                nc.sync.dma_start(out_rows[:, t, c], res[t][:, c])

@@ -17,209 +17,195 @@ ALU = mybir.AluOpType
 ACT = mybir.ActivationFunctionType
 
 P = 128
-PACK = 4
+PLANES = 4
 HALF = S // 2
-LIST_COLS = S // 16
+STRIPE = 16
+QUADRANTS = 4
+MX_ALIGN = 64
+PLANES_COPIED_BY_VECTOR = 2
 
 
 def tile_picked_skippullbfrac_none_p_kernel(tc, x_words, x_scales, w1, gn, w2, offs, n1, n2, n3, n4, out):
     nc = tc.nc
     with ExitStack() as ctx:
-        keep = ctx.enter_context(tc.tile_pool(name="keep", bufs=1))
+        sbuf = ctx.enter_context(tc.tile_pool(name="sbuf", bufs=1))
         psum = ctx.enter_context(tc.psum_pool(name="psum", bufs=1))
 
+        def places(half):
+            return slice(half * HALF, (half + 1) * HALF)
+
+        def entries(list_tile, half):
+            return list_tile[:, half * HALF // STRIPE : (half + 1) * HALF // STRIPE]
+
         def load_list(src, name):
-            tile = keep.tile([P, LIST_COLS], U16, name=name)
+            tile = sbuf.tile([P, S // STRIPE], U16, name=name)
             nc.sync.dma_start(tile[:], src)
             return tile
 
-        def cols(half):
-            return slice(half * HALF, (half + 1) * HALF)
+        def load_weight_half(weight, half, staged):
+            rows = weight.rearrange("(p j) c -> p j c", j=PLANES)
+            nc.sync.dma_start(staged[:], rows[:, :, places(half)])
 
-        def entries(tile, half):
-            return tile[:, half * HALF // 16 : (half + 1) * HALF // 16]
+        def round_weight_half(copy, staged, half, rounded):
+            dealt = rounded[:].rearrange("p (t m j) -> p m t j", t=PLANES, j=PLANES)
+            copy(out=dealt[:, half * P // 2 : (half + 1) * P // 2, :, :], in_=staged[:].rearrange("p j (m t) -> p m t j", t=PLANES))
 
-        xs_all = keep.tile([P, T], U8, name="xs_all")
-        nc.vector.memset(xs_all[:].bitcast(I32), 0)
-        offs_t = load_list(offs, "offs_t")
-        w1_raw = [keep.tile([P, PACK, H // 2], F32, name="w1_raw%d" % c) for c in range(2)]
-        w1_rows = w1.rearrange("(p j) c -> p j c", j=PACK)
-        for c in range(2):
-            nc.sync.dma_start(w1_raw[c][:], w1_rows[:, :, c * (H // 2) : (c + 1) * (H // 2)])
-        for q in range(4):
-            nc.sync.dma_start(xs_all[32 * q : 32 * q + 4, :].bitcast(I32), x_scales[0, 4 * q : 4 * q + 4, :].bitcast(I32))
-        xw_all = keep.tile([P, T], I32, name="xw_all")
-        nc.sync.dma_start(xw_all[:], x_words[0].rearrange("p c r -> p (c r)").bitcast(I32))
-        n2_t = load_list(n2, "n2_t")
-        n1_t = load_list(n1, "n1_t")
-        n4_t = load_list(n4, "n4_t")
-        gn_t = keep.tile([P, PACK], F32, name="gn_t")
-        nc.sync.dma_start(gn_t[:], gn.rearrange("(p t) o -> p (t o)", t=PACK))
-        w2_raw = [keep.tile([P, PACK, N // 2], F32, name="w2_raw%d" % c, tag="w2_raw") for c in range(1)]
-        w2_rows = w2.rearrange("(p j) c -> p j c", j=PACK)
-        nc.sync.dma_start(w2_raw[0][:], w2_rows[:, :, : N // 2])
-        n3_t = load_list(n3, "n3_t")
-
-        w1_bf = keep.tile([P, H * PACK], BF16, name="w1_bf", align_bytes=64)
-        w1_dealt = w1_bf[:].rearrange("p (t m j) -> p m t j", t=PACK, j=PACK)
-        for c in range(2):
-            nc.vector.tensor_copy(out=w1_dealt[:, c * 64 : (c + 1) * 64, :, :], in_=w1_raw[c][:].rearrange("p j (m t) -> p m t j", t=PACK))
-        xs_g = keep.tile([P, S], U8, name="xs_g", align_bytes=64)
-        nc.vector.tensor_copy(out=xs_g[:], in_=xs_all[:].indirect(offs_t[:]))
-        w1_q = keep.tile([P, H], U32, name="w1_q", tag="row0", align_bytes=64)
-        w1_s = keep.tile([P, H], U8, name="w1_s", tag="row1", align_bytes=64)
-        nc.vector.quantize_mx(out=w1_q[:].bitcast(FP8X4), scales=w1_s[:], in_=w1_bf[:])
-        xw_g = [keep.tile([P, HALF], U32, name="xw_g%d" % c, align_bytes=64) for c in range(2)]
-        y_win = [keep.tile([P, S], F32, name="y_win%d" % t) for t in range(PACK)]
-        y_cp = keep.tile([P, PACK, S], F32, name="y_cp")
-        for half in range(2):
-            nc.vector.tensor_copy(out=xw_g[half][:], in_=xw_all[:].bitcast(U32).indirect(entries(offs_t, half)))
-        for t, half in ((0, 0), (1, 0), (0, 1), (1, 1), (2, 0), (2, 1), (3, 0), (3, 1)):
-            bank = psum.tile([P, HALF], F32, name="y_bank", tag=("turn%d" % t if half == 0 else "side%d" % t))
+        def product(bank, w_words, w_scales, t, words, scales):
             m = slice(t * P, (t + 1) * P)
-            nc.tensor.matmul_mx(out=bank[:], lhsT=w1_q[:, m].bitcast(FP8X4), lhsT_scale=w1_s[:, m], rhs=xw_g[half][:].bitcast(FP8X4), rhs_scale=xs_g[:, cols(half)], start=True, stop=True)
-            nc.scalar.copy(out=y_win[t][:, cols(half)], in_=bank[:])
+            nc.tensor.matmul_mx(out=bank, lhsT=w_words[:, m].bitcast(FP8X4), lhsT_scale=w_scales[:, m], rhs=words.bitcast(FP8X4), rhs_scale=scales, start=True, stop=True)
 
-        ident = keep.tile([P, P], F32, name="ident")
-        make_identity(nc, ident[:])
-        neg_gn = keep.tile([P, PACK], F32, name="neg_gn")
-        nc.vector.tensor_scalar(out=neg_gn[:], in0=gn_t[:], scalar1=-1.0, scalar2=None, op0=ALU.mult)
+        table_scales = sbuf.tile([P, T], U8, name="table_scales")
+        nc.vector.memset(table_scales[:].bitcast(I32), 0)
+        offs_list = load_list(offs, "offs_list")
+        w1_staged = [sbuf.tile([P, PLANES, HALF], F32, name="w1_staged%d" % half) for half in range(2)]
+        load_weight_half(w1, 0, w1_staged[0])
+        for q in range(QUADRANTS):
+            nc.sync.dma_start(table_scales[32 * q : 32 * q + 4, :].bitcast(I32), x_scales[0, 4 * q : 4 * q + 4, :].bitcast(I32))
+        load_weight_half(w1, 1, w1_staged[1])
+        table_words = sbuf.tile([P, T], I32, name="table_words")
+        nc.sync.dma_start(table_words[:], x_words[0].rearrange("p c r -> p (c r)").bitcast(I32))
+        w2_staged = sbuf.tile([P, PLANES, HALF], F32, name="w2_staged", tag="w2_staged")
+        load_weight_half(w2, 0, w2_staged)
+        n2_list = load_list(n2, "n2_list")
+        n4_list = load_list(n4, "n4_list")
+        n1_list = load_list(n1, "n1_list")
+        gain = sbuf.tile([P, PLANES], F32, name="gain")
+        nc.sync.dma_start(gain[:], gn.rearrange("(p t) o -> p (t o)", t=PLANES))
+        n3_list = load_list(n3, "n3_list")
 
-        d1 = keep.tile([P, PACK, S], F32, name="d1")
-        d2 = keep.tile([P, PACK, S], F32, name="d2")
-        d4 = [keep.tile([P, S], F32, name="d4", tag="row%d" % t, align_bytes=64) for t in range(PACK)]
-        mag = [keep.tile([P, PACK, HALF], F32, name="mag", tag="mag%d" % c, align_bytes=64) for c in range(2)]
-        root = [keep.tile([P, PACK, HALF], F32, name="root", tag="root%d" % c) for c in range(2)]
-        half_bias = keep.tile([P, 1], F32, name="half_bias")
-        nc.vector.memset(half_bias[:], 0.5)
+        w1_rounded = sbuf.tile([P, H * PLANES], BF16, name="w1_rounded", align_bytes=MX_ALIGN)
+        for half in range(2):
+            round_weight_half(nc.vector.tensor_copy, w1_staged[half], half, w1_rounded)
+        picked_scales = sbuf.tile([P, S], U8, name="picked_scales", align_bytes=MX_ALIGN)
+        nc.vector.tensor_copy(out=picked_scales[:], in_=table_scales[:].indirect(offs_list[:]))
+        w1_words = sbuf.tile([P, H], U32, name="w1_words", tag="row0", align_bytes=MX_ALIGN)
+        w1_scales = sbuf.tile([P, H], U8, name="w1_scales", tag="row1", align_bytes=MX_ALIGN)
+        nc.vector.quantize_mx(out=w1_words[:].bitcast(FP8X4), scales=w1_scales[:], in_=w1_rounded[:])
+        picked_words = [sbuf.tile([P, HALF], U32, name="picked_words%d" % half, align_bytes=MX_ALIGN) for half in range(2)]
+        for half in range(2):
+            nc.vector.tensor_copy(out=picked_words[half][:], in_=table_words[:].bitcast(U32).indirect(entries(offs_list, half)))
 
-        warm = keep.tile([P, 1], F32, name="warm")
-        nc.scalar.activation(out=warm[:], in_=half_bias[:], func=ACT.Abs_reciprocal_sqrt)
+        y = [sbuf.tile([P, S], F32, name="y%d" % t) for t in range(PLANES)]
+        steps = [(t, half) for half in range(2) for t in range(2)] + [(t, half) for t in range(2, PLANES) for half in range(2)]
+        for t, half in steps:
+            y_bank = psum.tile([P, HALF], F32, name="y_bank", tag=("low%d" if half == 0 else "high%d") % t)
+            product(y_bank[:], w1_words, w1_scales, t, picked_words[half][:], picked_scales[:, places(half)])
+            nc.scalar.copy(out=y[t][:, places(half)], in_=y_bank[:])
 
-        def diff(dst, lst, t, half):
-            nc.vector.tensor_tensor(out=dst[:, t, cols(half)], in0=y_win[t][:].indirect(entries(lst, half)), in1=y_cp[:, t, cols(half)], op=ALU.subtract)
+        identity = sbuf.tile([P, P], F32, name="identity")
+        make_identity(nc, identity[:])
+        minus_gain = sbuf.tile([P, PLANES], F32, name="minus_gain")
+        nc.vector.tensor_scalar(out=minus_gain[:], in0=gain[:], scalar1=-1.0, scalar2=None, op0=ALU.mult)
+        one_half = sbuf.tile([P, 1], F32, name="one_half")
+        nc.vector.memset(one_half[:], 0.5)
 
-        def fetch4(pair):
-            for t, half in ((2 * pair, 0), (2 * pair, 1), (2 * pair + 1, 0), (2 * pair + 1, 1)):
-                nc.scalar.activation(out=d4[t][:, cols(half)], in_=y_win[t][:].indirect(entries(n4_t, half)), func=ACT.Copy, scale=-1.0)
+        unread = sbuf.tile([P, 1], F32, name="unread")
+        nc.scalar.activation(out=unread[:], in_=one_half[:], func=ACT.Abs_reciprocal_sqrt)
 
-        def denominators(half):
-            nc.scalar.activation(out=mag[half][:], in_=d2[:, :, cols(half)], func=ACT.Abs)
-            nc.scalar.activation(out=root[half][:], in_=mag[half][:], func=ACT.Abs_reciprocal_sqrt, bias=half_bias[:])
+        y_again = sbuf.tile([P, PLANES, S], F32, name="y_again")
+        for half in range(2):
+            for t in range(PLANES):
+                if half == 0 or t < PLANES_COPIED_BY_VECTOR:
+                    nc.vector.tensor_copy(out=y_again[:, t, places(half)], in_=y[t][:, places(half)])
+                else:
+                    nc.sync.dma_start(y_again[:, t, places(half)], y[t][:, places(half)])
 
-        z_bf = [keep.tile([P, HALF * PACK], BF16, name="z_bf%d" % c, align_bytes=64) for c in range(2)]
-        z_q = [keep.tile([P, HALF], U32, name="z_q%d" % c, align_bytes=64) for c in range(2)]
-        z_s = [keep.tile([P, HALF], U8, name="z_s%d" % c, align_bytes=64) for c in range(2)]
+        def differences(dst, list_tile, half):
+            for t in range(PLANES):
+                nc.vector.tensor_tensor(out=dst[:, t, places(half)], in0=y[t][:].indirect(entries(list_tile, half)), in1=y_again[:, t, places(half)], op=ALU.subtract)
 
-        def make_z(half):
-            for t in range(PACK):
-                nc.vector.scalar_tensor_tensor(out=d1[:, t, cols(half)], in0=d1[:, t, cols(half)], scalar=neg_gn[:, t : t + 1], in1=root[half][:, t, :], op0=ALU.mult, op1=ALU.mult)
+        spread = sbuf.tile([P, PLANES, S], F32, name="spread")
+        magnitude = [sbuf.tile([P, PLANES, HALF], F32, name="magnitude", tag="magnitude%d" % half) for half in range(2)]
+        inv_root = [sbuf.tile([P, PLANES, HALF], F32, name="inv_root%d" % half) for half in range(2)]
+
+        def inverse_roots(half):
+            differences(spread, n2_list, half)
+            nc.scalar.activation(out=magnitude[half][:], in_=spread[:, :, places(half)], func=ACT.Abs)
+            nc.scalar.activation(out=inv_root[half][:], in_=magnitude[half][:], func=ACT.Abs_reciprocal_sqrt, bias=one_half[:])
+
+        z_rounded = [sbuf.tile([P, HALF * PLANES], BF16, name="z_rounded%d" % half, align_bytes=MX_ALIGN) for half in range(2)]
+        z_words = [sbuf.tile([P, HALF], U32, name="z_words%d" % half, align_bytes=MX_ALIGN) for half in range(2)]
+        z_scales = [sbuf.tile([P, HALF], U8, name="z_scales%d" % half, align_bytes=MX_ALIGN) for half in range(2)]
+
+        def round_z(numerator, half):
+            for t in range(PLANES):
+                part = numerator[:, t, places(half)]
+                nc.vector.scalar_tensor_tensor(out=part, in0=part, scalar=minus_gain[:, t : t + 1], in1=inv_root[half][:, t, :], op0=ALU.mult, op1=ALU.mult)
             nc.vector.tensor_tensor(
-                out=z_bf[half][:].rearrange("p (c i t) -> p c t i", i=4, t=PACK),
-                in0=d1[:, :, cols(half)].rearrange("p t (c i) -> p c t i", i=4),
-                in1=root[half][:].rearrange("p t (c i) -> p c t i", i=4),
+                out=z_rounded[half][:].rearrange("p (c i t) -> p c t i", i=4, t=PLANES),
+                in0=numerator[:, :, places(half)].rearrange("p t (c i) -> p c t i", i=4),
+                in1=inv_root[half][:].rearrange("p t (c i) -> p c t i", i=4),
                 op=ALU.mult,
             )
 
         def quantise_z(half):
-            if half == 1:
-                z_q[half] = keep.tile([P, HALF], U32, name="z_q_late", tag="mag1", align_bytes=64)
-            nc.vector.quantize_mx(out=z_q[half][:].bitcast(FP8X4), scales=z_s[half][:], in_=z_bf[half][:])
+            nc.vector.quantize_mx(out=z_words[half][:].bitcast(FP8X4), scales=z_scales[half][:], in_=z_rounded[half][:])
 
-        w2_bf = keep.tile([P, N * PACK], BF16, name="w2_bf", align_bytes=64)
-        w2_q = keep.tile([P, N], U32, name="w2_q", align_bytes=64)
-        w2_s = keep.tile([P, N], U8, name="w2_s", align_bytes=64)
-        h_win = []
-        h_bank = {}
+        first_numerator = sbuf.tile([P, PLANES, HALF], F32, name="first_numerator")
+        inverse_roots(0)
+        differences(first_numerator, n1_list, 0)
+        inverse_roots(1)
 
-        def second_product(half):
-            per_bank = 2 - half
-            for first in range(0, PACK, per_bank):
-                bank = psum.tile([P, per_bank, HALF], F32, name="h_bank", tag="side%d" % (first // 2 if half == 0 else (first + 2) % PACK))
-                for i in range(per_bank):
-                    m = slice((first + i) * P, (first + i + 1) * P)
-                    nc.tensor.matmul_mx(out=bank[:, i, :], lhsT=w2_q[:, m].bitcast(FP8X4), lhsT_scale=w2_s[:, m], rhs=z_q[half][:].bitcast(FP8X4), rhs_scale=z_s[half][:], start=True, stop=True)
-                for i in range(per_bank):
-                    move = nc.vector.tensor_copy if half == 1 and first < 2 else nc.scalar.copy
-                    move(out=h_win[first + i][:, cols(half)], in_=bank[:, i, :])
-
-        def negate(t, half):
-            if half == 0:
-                nc.vector.tensor_copy(out=y_cp[:, t, cols(half)], in_=y_win[t][:, cols(half)])
-            else:
-                nc.sync.dma_start(y_cp[:, t, cols(half)], y_win[t][:, cols(half)])
-
-        gate = []
-
-        def make_gate(t, gate_t):
-            turned = psum.tile([P, S], F32, name="turned", tag="turn%d" % t)
-            for k, src in enumerate((y_win[t], d4[t])):
-                for b in range(S // P):
-                    blk = slice(b * P, (b + 1) * P)
-                    nc.tensor.matmul(out=turned[:, blk], lhsT=src[:, blk], rhs=ident[:], start=(k == 0 and b == 0), stop=(k == 1 and b == S // P - 1), is_transpose=True)
-            nc.scalar.activation(out=gate_t[:, t % 2, :], in_=turned[:], func=ACT.Sigmoid, scale=-1.0)
-            back = psum.tile([P, S], F32, name="gate", tag="turn%d" % t)
-            for b in range(S // P):
-                blk = slice(b * P, (b + 1) * P)
-                nc.tensor.transpose(back[:, blk], gate_t[:, t % 2, blk], ident[:])
-            gate.append(back)
-
-        for t in range(PACK):
-            negate(t, 0)
-        for t in range(PACK):
-            negate(t, 1)
-        for t in range(PACK):
-            diff(d2, n2_t, t, 0)
-        denominators(0)
-        for t in range(PACK):
-            diff(d1, n1_t, t, 0)
-        for t in range(PACK):
-            diff(d2, n2_t, t, 1)
-        denominators(1)
-        fetch4(0)
-        fetch4(1)
-        w2_dealt = w2_bf[:].rearrange("p (t m j) -> p m t j", t=PACK, j=PACK)
-        for c, move in enumerate((nc.vector.tensor_copy, nc.scalar.copy)):
-            if c == 1:
-                w2_raw.append(keep.tile([P, PACK, N // 2], F32, name="w2_raw1", tag="w2_raw"))
-                nc.sync.dma_start(w2_raw[1][:], w2_rows[:, :, N // 2 :])
-            move(out=w2_dealt[:, c * 64 : (c + 1) * 64, :, :], in_=w2_raw[c][:].rearrange("p j (m t) -> p m t j", t=PACK))
-        make_z(0)
-        nc.vector.quantize_mx(out=w2_q[:].bitcast(FP8X4), scales=w2_s[:], in_=w2_bf[:])
-        quantise_z(0)
-        for t in range(PACK):
-            diff(d1, n1_t, t, 1)
-        make_z(1)
-        early = keep.tile([P, 2, S], F32, name="gate_t", tag="mag1", align_bytes=64)
-        for t in range(2):
-            make_gate(t, early)
-        for t in range(PACK):
-            h_win.append(keep.tile([P, S], F32, name="h_win", tag="win%d" % t))
-        second_product(0)
-        quantise_z(1)
-        second_product(1)
-        late = keep.tile([P, 2, S], F32, name="gate_t", tag="root1")
-        for t in range(2, PACK):
-            make_gate(t, late)
-
-        stay = keep.tile([P, PACK, S], F32, name="stay")
-        for half in range(2):
-            for t in range(PACK):
-                nc.vector.scalar_tensor_tensor(out=stay[:, t, cols(half)], in0=gate[t][:, cols(half)], scalar=1.0, in1=h_win[t][:, cols(half)], op0=ALU.subtract, op1=ALU.mult)
-        pull = keep.tile([P, PACK, S], F32, name="pull")
-        res = [keep.tile([P, S], F32, name="res%d" % t) for t in range(PACK)]
-        out_rows = out.rearrange("(p t) c -> p t c", t=PACK)
-        for t in range(PACK):
+        minus_y4 = [sbuf.tile([P, S], F32, name="minus_y4", tag="row%d" % t, align_bytes=MX_ALIGN) for t in range(PLANES)]
+        for t in range(PLANES):
             for half in range(2):
-                c = cols(half)
-                if t == -1:
-                    nc.vector.tensor_copy(out=pull[:, t, c], in_=h_win[t][:].indirect(entries(n3_t, half)))
-                else:
-                    nc.scalar.activation(out=pull[:, t, c], in_=h_win[t][:].indirect(entries(n3_t, half)), func=ACT.Copy)
-        for t in range(PACK):
-            for c in (cols(0), cols(1)):
-                nc.vector.tensor_tensor(out=pull[:, t, c], in0=pull[:, t, c], in1=gate[t][:, c], op=ALU.mult)
-            for c in (cols(0), cols(1)):
-                (nc.gpsimd if t in () else nc.vector).tensor_tensor(out=res[t][:, c], in0=pull[:, t, c], in1=stay[:, t, c], op=ALU.subtract)
-            for c in ((cols(0), cols(1)) if t >= 3 else (slice(0, S),)):
-                nc.sync.dma_start(out_rows[:, t, c], res[t][:, c])
+                nc.scalar.activation(out=minus_y4[t][:, places(half)], in_=y[t][:].indirect(entries(n4_list, half)), func=ACT.Copy, scale=-1.0)
+
+        w2_rounded = sbuf.tile([P, N * PLANES], BF16, name="w2_rounded", align_bytes=MX_ALIGN)
+        round_weight_half(nc.vector.tensor_copy, w2_staged, 0, w2_rounded)
+        w2_restaged = sbuf.tile([P, PLANES, HALF], F32, name="w2_restaged", tag="w2_staged")
+        load_weight_half(w2, 1, w2_restaged)
+        round_weight_half(nc.scalar.copy, w2_restaged, 1, w2_rounded)
+
+        round_z(first_numerator, 0)
+        w2_words = sbuf.tile([P, N], U32, name="w2_words", align_bytes=MX_ALIGN)
+        w2_scales = sbuf.tile([P, N], U8, name="w2_scales", align_bytes=MX_ALIGN)
+        nc.vector.quantize_mx(out=w2_words[:].bitcast(FP8X4), scales=w2_scales[:], in_=w2_rounded[:])
+        quantise_z(0)
+        differences(spread, n1_list, 1)
+        round_z(spread, 1)
+
+        blocks = [slice(b * P, (b + 1) * P) for b in range(S // P)]
+        gate_turned = sbuf.tile([P, PLANES, S], F32, name="gate_turned", tag="magnitude1")
+        gate = []
+        for t in range(PLANES):
+            turned = psum.tile([P, S], F32, name="turned", tag="low%d" % t)
+            passes = [(term, block) for term in (y[t], minus_y4[t]) for block in blocks]
+            for i, (term, block) in enumerate(passes):
+                nc.tensor.matmul(out=turned[:, block], lhsT=term[:, block], rhs=identity[:], start=(i == 0), stop=(i == len(passes) - 1), is_transpose=True)
+            nc.scalar.activation(out=gate_turned[:, t, :], in_=turned[:], func=ACT.Sigmoid, scale=-1.0)
+            gate_bank = psum.tile([P, S], F32, name="gate_bank", tag="low%d" % t)
+            for block in blocks:
+                nc.tensor.transpose(gate_bank[:, block], gate_turned[:, t, block], identity[:])
+            gate.append(gate_bank)
+
+        h = [sbuf.tile([P, S], F32, name="h%d" % t) for t in range(PLANES)]
+        for pair in range(PLANES // 2):
+            pair_bank = psum.tile([P, 2, HALF], F32, name="pair_bank", tag="high%d" % pair)
+            for i in range(2):
+                product(pair_bank[:, i, :], w2_words, w2_scales, 2 * pair + i, z_words[0][:], z_scales[0][:])
+            for i in range(2):
+                nc.scalar.copy(out=h[2 * pair + i][:, places(0)], in_=pair_bank[:, i, :])
+        quantise_z(1)
+        for t in range(PLANES):
+            h_bank = psum.tile([P, HALF], F32, name="h_bank", tag="high%d" % ((t + 2) % PLANES))
+            product(h_bank[:], w2_words, w2_scales, t, z_words[1][:], z_scales[1][:])
+            nc.scalar.copy(out=h[t][:, places(1)], in_=h_bank[:])
+
+        stay = sbuf.tile([P, PLANES, S], F32, name="stay")
+        for half in range(2):
+            for t in range(PLANES):
+                nc.vector.scalar_tensor_tensor(out=stay[:, t, places(half)], in0=gate[t][:, places(half)], scalar=1.0, in1=h[t][:, places(half)], op0=ALU.subtract, op1=ALU.mult)
+        pull = sbuf.tile([P, PLANES, S], F32, name="pull")
+        for t in range(PLANES):
+            for half in range(2):
+                nc.scalar.activation(out=pull[:, t, places(half)], in_=h[t][:].indirect(entries(n3_list, half)), func=ACT.Copy)
+        out_planes = out.rearrange("(p t) c -> p t c", t=PLANES)
+        for t in range(PLANES):
+            result = sbuf.tile([P, S], F32, name="result%d" % t)
+            for half in range(2):
+                nc.vector.tensor_tensor(out=pull[:, t, places(half)], in0=pull[:, t, places(half)], in1=gate[t][:, places(half)], op=ALU.mult)
+            for half in range(2):
+                nc.vector.tensor_tensor(out=result[:, places(half)], in0=pull[:, t, places(half)], in1=stay[:, t, places(half)], op=ALU.subtract)
+            for part in ([places(0), places(1)] if t == PLANES - 1 else [slice(0, S)]):
+                nc.sync.dma_start(out_planes[:, t, part], result[:, part])

from contextlib import ExitStack

import concourse.mybir as mybir
from concourse.masks import make_identity

K, T, S, N, H = 512, 2048, 512, 512, 512
FLOPS = 2 * K * H * S + 2 * H * N * S

F32 = mybir.dt.float32
BF16 = mybir.dt.bfloat16
I32 = mybir.dt.int32
U32 = mybir.dt.uint32
U16 = mybir.dt.uint16
U8 = mybir.dt.uint8
FP8X4 = mybir.dt.float8_e4m3fn_x4
ALU = mybir.AluOpType
ACT = mybir.ActivationFunctionType

P = 128
PLANES = 4
HALF = S // 2
STRIPE = 16
QUADRANTS = 4
MX_ALIGN = 64
PLANES_COPIED_BY_VECTOR = 2


def tile_picked_skippullbfrac_none_p_kernel(tc, x_words, x_scales, w1, gn, w2, offs, n1, n2, n3, n4, out):
    nc = tc.nc
    with ExitStack() as ctx:
        sbuf = ctx.enter_context(tc.tile_pool(name="sbuf", bufs=1))
        psum = ctx.enter_context(tc.psum_pool(name="psum", bufs=1))

        def places(half):
            return slice(half * HALF, (half + 1) * HALF)

        def entries(list_tile, half):
            return list_tile[:, half * HALF // STRIPE : (half + 1) * HALF // STRIPE]

        def load_list(src, name):
            tile = sbuf.tile([P, S // STRIPE], U16, name=name)
            nc.sync.dma_start(tile[:], src)
            return tile

        def load_weight_half(weight, half, staged):
            rows = weight.rearrange("(p j) c -> p j c", j=PLANES)
            nc.sync.dma_start(staged[:], rows[:, :, places(half)])

        def round_weight_half(copy, staged, half, rounded):
            dealt = rounded[:].rearrange("p (t m j) -> p m t j", t=PLANES, j=PLANES)
            copy(out=dealt[:, half * P // 2 : (half + 1) * P // 2, :, :], in_=staged[:].rearrange("p j (m t) -> p m t j", t=PLANES))

        def product(bank, w_words, w_scales, t, words, scales):
            m = slice(t * P, (t + 1) * P)
            nc.tensor.matmul_mx(out=bank, lhsT=w_words[:, m].bitcast(FP8X4), lhsT_scale=w_scales[:, m], rhs=words.bitcast(FP8X4), rhs_scale=scales, start=True, stop=True)

        table_scales = sbuf.tile([P, T], U8, name="table_scales")
        nc.vector.memset(table_scales[:].bitcast(I32), 0)
        offs_list = load_list(offs, "offs_list")
        w1_staged = [sbuf.tile([P, PLANES, HALF], F32, name="w1_staged%d" % half) for half in range(2)]
        load_weight_half(w1, 0, w1_staged[0])
        for q in range(QUADRANTS):
            nc.sync.dma_start(table_scales[32 * q : 32 * q + 4, :].bitcast(I32), x_scales[0, 4 * q : 4 * q + 4, :].bitcast(I32))
        load_weight_half(w1, 1, w1_staged[1])
        table_words = sbuf.tile([P, T], I32, name="table_words")
        nc.sync.dma_start(table_words[:], x_words[0].rearrange("p c r -> p (c r)").bitcast(I32))
        w2_staged = sbuf.tile([P, PLANES, HALF], F32, name="w2_staged", tag="w2_staged")
        load_weight_half(w2, 0, w2_staged)
        n2_list = load_list(n2, "n2_list")
        n4_list = load_list(n4, "n4_list")
        n1_list = load_list(n1, "n1_list")
        gain = sbuf.tile([P, PLANES], F32, name="gain")
        nc.sync.dma_start(gain[:], gn.rearrange("(p t) o -> p (t o)", t=PLANES))
        n3_list = load_list(n3, "n3_list")

        w1_rounded = sbuf.tile([P, H * PLANES], BF16, name="w1_rounded", align_bytes=MX_ALIGN)
        for half in range(2):
            round_weight_half(nc.vector.tensor_copy, w1_staged[half], half, w1_rounded)
        picked_scales = sbuf.tile([P, S], U8, name="picked_scales", align_bytes=MX_ALIGN)
        nc.vector.tensor_copy(out=picked_scales[:], in_=table_scales[:].indirect(offs_list[:]))
        w1_words = sbuf.tile([P, H], U32, name="w1_words", tag="row0", align_bytes=MX_ALIGN)
        w1_scales = sbuf.tile([P, H], U8, name="w1_scales", tag="row1", align_bytes=MX_ALIGN)
        nc.vector.quantize_mx(out=w1_words[:].bitcast(FP8X4), scales=w1_scales[:], in_=w1_rounded[:])
        picked_words = [sbuf.tile([P, HALF], U32, name="picked_words%d" % half, align_bytes=MX_ALIGN) for half in range(2)]
        for half in range(2):
            nc.vector.tensor_copy(out=picked_words[half][:], in_=table_words[:].bitcast(U32).indirect(entries(offs_list, half)))

        y = [sbuf.tile([P, S], F32, name="y%d" % t) for t in range(PLANES)]
        steps = [(t, half) for half in range(2) for t in range(2)] + [(t, half) for t in range(2, PLANES) for half in range(2)]
        for t, half in steps:
            y_bank = psum.tile([P, HALF], F32, name="y_bank", tag=("low%d" if half == 0 else "high%d") % t)
            product(y_bank[:], w1_words, w1_scales, t, picked_words[half][:], picked_scales[:, places(half)])
            nc.scalar.copy(out=y[t][:, places(half)], in_=y_bank[:])

        identity = sbuf.tile([P, P], F32, name="identity")
        make_identity(nc, identity[:])
        minus_gain = sbuf.tile([P, PLANES], F32, name="minus_gain")
        nc.vector.tensor_scalar(out=minus_gain[:], in0=gain[:], scalar1=-1.0, scalar2=None, op0=ALU.mult)
        one_half = sbuf.tile([P, 1], F32, name="one_half")
        nc.vector.memset(one_half[:], 0.5)

        unread = sbuf.tile([P, 1], F32, name="unread")
        nc.scalar.activation(out=unread[:], in_=one_half[:], func=ACT.Abs_reciprocal_sqrt)

        y_again = sbuf.tile([P, PLANES, S], F32, name="y_again")
        for half in range(2):
            for t in range(PLANES):
                if half == 0 or t < PLANES_COPIED_BY_VECTOR:
                    nc.vector.tensor_copy(out=y_again[:, t, places(half)], in_=y[t][:, places(half)])
                else:
                    nc.sync.dma_start(y_again[:, t, places(half)], y[t][:, places(half)])

        def differences(dst, list_tile, half):
            for t in range(PLANES):
                nc.vector.tensor_tensor(out=dst[:, t, places(half)], in0=y[t][:].indirect(entries(list_tile, half)), in1=y_again[:, t, places(half)], op=ALU.subtract)

        spread = sbuf.tile([P, PLANES, S], F32, name="spread")
        magnitude = [sbuf.tile([P, PLANES, HALF], F32, name="magnitude", tag="magnitude%d" % half) for half in range(2)]
        inv_root = [sbuf.tile([P, PLANES, HALF], F32, name="inv_root%d" % half) for half in range(2)]

        def inverse_roots(half):
            differences(spread, n2_list, half)
            nc.scalar.activation(out=magnitude[half][:], in_=spread[:, :, places(half)], func=ACT.Abs)
            nc.scalar.activation(out=inv_root[half][:], in_=magnitude[half][:], func=ACT.Abs_reciprocal_sqrt, bias=one_half[:])

        z_rounded = [sbuf.tile([P, HALF * PLANES], BF16, name="z_rounded%d" % half, align_bytes=MX_ALIGN) for half in range(2)]
        z_words = [sbuf.tile([P, HALF], U32, name="z_words%d" % half, align_bytes=MX_ALIGN) for half in range(2)]
        z_scales = [sbuf.tile([P, HALF], U8, name="z_scales%d" % half, align_bytes=MX_ALIGN) for half in range(2)]

        def round_z(numerator, half):
            for t in range(PLANES):
                part = numerator[:, t, places(half)]
                nc.vector.scalar_tensor_tensor(out=part, in0=part, scalar=minus_gain[:, t : t + 1], in1=inv_root[half][:, t, :], op0=ALU.mult, op1=ALU.mult)
            nc.vector.tensor_tensor(
                out=z_rounded[half][:].rearrange("p (c i t) -> p c t i", i=4, t=PLANES),
                in0=numerator[:, :, places(half)].rearrange("p t (c i) -> p c t i", i=4),
                in1=inv_root[half][:].rearrange("p t (c i) -> p c t i", i=4),
                op=ALU.mult,
            )

        def quantise_z(half):
            nc.vector.quantize_mx(out=z_words[half][:].bitcast(FP8X4), scales=z_scales[half][:], in_=z_rounded[half][:])

        first_numerator = sbuf.tile([P, PLANES, HALF], F32, name="first_numerator")
        inverse_roots(0)
        differences(first_numerator, n1_list, 0)
        inverse_roots(1)

        minus_y4 = [sbuf.tile([P, S], F32, name="minus_y4", tag="row%d" % t, align_bytes=MX_ALIGN) for t in range(PLANES)]
        for t in range(PLANES):
            for half in range(2):
                nc.scalar.activation(out=minus_y4[t][:, places(half)], in_=y[t][:].indirect(entries(n4_list, half)), func=ACT.Copy, scale=-1.0)

        w2_rounded = sbuf.tile([P, N * PLANES], BF16, name="w2_rounded", align_bytes=MX_ALIGN)
        round_weight_half(nc.vector.tensor_copy, w2_staged, 0, w2_rounded)
        w2_restaged = sbuf.tile([P, PLANES, HALF], F32, name="w2_restaged", tag="w2_staged")
        load_weight_half(w2, 1, w2_restaged)
        round_weight_half(nc.scalar.copy, w2_restaged, 1, w2_rounded)

        round_z(first_numerator, 0)
        w2_words = sbuf.tile([P, N], U32, name="w2_words", align_bytes=MX_ALIGN)
        w2_scales = sbuf.tile([P, N], U8, name="w2_scales", align_bytes=MX_ALIGN)
        nc.vector.quantize_mx(out=w2_words[:].bitcast(FP8X4), scales=w2_scales[:], in_=w2_rounded[:])
        quantise_z(0)
        differences(spread, n1_list, 1)
        round_z(spread, 1)

        blocks = [slice(b * P, (b + 1) * P) for b in range(S // P)]
        gate_turned = sbuf.tile([P, PLANES, S], F32, name="gate_turned", tag="magnitude1")
        gate = []
        for t in range(PLANES):
            turned = psum.tile([P, S], F32, name="turned", tag="low%d" % t)
            passes = [(term, block) for term in (y[t], minus_y4[t]) for block in blocks]
            for i, (term, block) in enumerate(passes):
                nc.tensor.matmul(out=turned[:, block], lhsT=term[:, block], rhs=identity[:], start=(i == 0), stop=(i == len(passes) - 1), is_transpose=True)
            nc.scalar.activation(out=gate_turned[:, t, :], in_=turned[:], func=ACT.Sigmoid, scale=-1.0)
            gate_bank = psum.tile([P, S], F32, name="gate_bank", tag="low%d" % t)
            for block in blocks:
                nc.tensor.transpose(gate_bank[:, block], gate_turned[:, t, block], identity[:])
            gate.append(gate_bank)

        h = [sbuf.tile([P, S], F32, name="h%d" % t) for t in range(PLANES)]
        for pair in range(PLANES // 2):
            pair_bank = psum.tile([P, 2, HALF], F32, name="pair_bank", tag="high%d" % pair)
            for i in range(2):
                product(pair_bank[:, i, :], w2_words, w2_scales, 2 * pair + i, z_words[0][:], z_scales[0][:])
            for i in range(2):
                nc.scalar.copy(out=h[2 * pair + i][:, places(0)], in_=pair_bank[:, i, :])
        quantise_z(1)
        for t in range(PLANES):
            h_bank = psum.tile([P, HALF], F32, name="h_bank", tag="high%d" % ((t + 2) % PLANES))
            product(h_bank[:], w2_words, w2_scales, t, z_words[1][:], z_scales[1][:])
            nc.scalar.copy(out=h[t][:, places(1)], in_=h_bank[:])

        stay = sbuf.tile([P, PLANES, S], F32, name="stay")
        for half in range(2):
            for t in range(PLANES):
                nc.vector.scalar_tensor_tensor(out=stay[:, t, places(half)], in0=gate[t][:, places(half)], scalar=1.0, in1=h[t][:, places(half)], op0=ALU.subtract, op1=ALU.mult)
        pull = sbuf.tile([P, PLANES, S], F32, name="pull")
        for t in range(PLANES):
            for half in range(2):
                nc.scalar.activation(out=pull[:, t, places(half)], in_=h[t][:].indirect(entries(n3_list, half)), func=ACT.Copy)
        out_planes = out.rearrange("(p t) c -> p t c", t=PLANES)
        for t in range(PLANES):
            result = sbuf.tile([P, S], F32, name="result%d" % t)
            for half in range(2):
                nc.vector.tensor_tensor(out=pull[:, t, places(half)], in0=pull[:, t, places(half)], in1=gate[t][:, places(half)], op=ALU.mult)
            for half in range(2):
                nc.vector.tensor_tensor(out=result[:, places(half)], in0=pull[:, t, places(half)], in1=stay[:, t, places(half)], op=ALU.subtract)
            for part in ([places(0), places(1)] if t == PLANES - 1 else [slice(0, S)]):
                nc.sync.dma_start(out_planes[:, t, part], result[:, part])
